import numpy as np, ml_dtypes
CORES = [66,74,82,90,194,202,210,218]
N = 8
import mx_ref
BF = ml_dtypes.bfloat16
def entries(a):
    return np.ascontiguousarray(a.T).reshape(-1)
def table(e):
    return np.ascontiguousarray(np.reshape(e, (-1, 16)).T).astype(np.int32)
def cols(t, e):
    v = np.concatenate([t.reshape(128, -1, 4), np.zeros((128, 1, 4), BF)], axis=1)
    return np.ascontiguousarray(v[:, e]).reshape(128, -1)
def f(rng, *shape):
    return mx_ref.flush((rng.standard_normal(shape, dtype=np.float32) * np.exp2(rng.integers(-2, 3, shape[:-1] + (1,)))).astype(BF))
def wide(rng, *shape, cols=0):
    v = rng.standard_normal(shape, dtype=np.float32) * np.exp2(rng.integers(-12, 13, shape)).astype(np.float32)
    if cols: v *= np.repeat(np.exp2(rng.integers(-cols, cols + 1, shape[:-2] + (1, shape[-1] // 4))) * (rng.random(shape[:-2] + (1, shape[-1] // 4)) > 0.0625), 4, axis=-1).astype(np.float32)
    return mx_ref.flush(v.astype(BF))
TA, TB, CI, CJ, JW = 256, 256, 32, 48, 384
SIDE = [0 if c < 128 else 1 for c in CORES]
GCOL = [SIDE[:r].count(SIDE[r]) for r in range(N)]
def fill(rng, total, cap, wd, first, back):
    n = np.zeros(N, int)
    for q in first: n[q] = min(cap, total - n.sum())
    while n.sum() < total:
        q = rng.integers(0, N)
        if n[q] < cap: n[q] += 1
    s, used = np.full((N, cap), -1), []
    for q in range(N):
        k, v = rng.permutation(cap)[:n[q]], rng.integers(0, wd, n[q])
        if back: k, v = np.sort(k), np.sort(v)[::-1]
        s[q, k] = v; used += list(q * cap + k)
    return s, (np.sort(used)[::-1] if back else rng.permutation(used))
def lists(rng, full=False, own=False, back=False, alike=False):
    A, B = [], []
    for i in range(2):
        A.append(fill(rng, 128, CI, TA, rng.permutation(N) if full else [r for r in range(N) if own and SIDE[r] == i], back))
    for k in range(4):
        B.append(fill(rng, JW, CJ, TB, rng.permutation(N) if full else [r for r in range(N) if own and GCOL[r] == k], back))
    if alike: B = [B[0]] * 4
    return {"sa": np.stack([table(np.concatenate([A[i][0][q] for i in range(2)])) for q in range(N)]),
            "sb": np.stack([table(np.concatenate([B[k][0][q] for k in range(4)])) for q in range(N)]),
            "pi": np.stack([table(A[SIDE[r]][1]) for r in range(N)]), "pj": np.stack([table(B[GCOL[r]][1]) for r in range(N)])}
def setup_inputs(rng):
    return {"a": f(rng, N, 128, 4 * TA), "b": f(rng, N, 128, 4 * TB), **lists(rng)}
def setup_inputs_alike(rng):
    return {**setup_inputs(rng), **lists(rng, alike=True)}
def setup_inputs_full(rng):
    return {**setup_inputs(rng), **lists(rng, full=True)}
def setup_inputs_own(rng):
    return {**setup_inputs(rng), **lists(rng, own=True)}
def setup_inputs_reversed(rng):
    return {**setup_inputs(rng), **lists(rng, back=True)}
def setup_inputs_spread(rng):
    d = setup_inputs(rng); d["a"], d["b"] = wide(rng, N, 128, 4 * TA, cols=6), wide(rng, N, 128, 4 * TB, cols=6); return d
def check_inputs(d):
    bad = []
    for s, p, wd, cap, total, place in (("sa", "pi", TA, CI, 128, SIDE), ("sb", "pj", TB, CJ, JW, GCOL)):
        e = np.stack([entries(d[s][q]) for q in range(N)])
        if e.min() < -1 or e.max() >= wd: bad.append(s)
        for r in range(N):
            v = e[:, cap * place[r]:cap * place[r] + cap].reshape(-1)
            if (v >= 0).sum() != total: bad.append(s + " count")
            t = entries(d[p][r])
            if t.min() < 0 or t.max() >= N * cap: bad.append(p); continue
            if len(set(t.tolist())) != total or (v[t] < 0).any(): bad.append(p + " slots")
            if (d[p][r] != d[p][place.index(place[r])]).any(): bad.append(p + " not the same")
    return bad
def reference(a, b, sa, sb, pi, pj):
    y = np.zeros((N, 128, JW), np.float32)
    for r in range(N):
        i, k = SIDE[r], GCOL[r]
        A = np.concatenate([cols(a[q], entries(sa[q])[CI * i:CI * i + CI]) for q in range(N)], axis=1)
        B = np.concatenate([cols(b[q], entries(sb[q])[CJ * k:CJ * k + CJ]) for q in range(N)], axis=1)
        y[r] = mx_ref.matmul(mx_ref.quantize(cols(A, entries(pi[r]))), mx_ref.quantize(cols(B, entries(pj[r]))))
    return {"y": y}

@@ -1,0 +1,252 @@
+from concourse.bass import DstId, RemoteDMATransfer, IndirectOffsetOnAxis
+from concourse.mybir import dt, AluOpType, AxisListType, ActivationFunctionType
+
+N, NC, CI, CJ, JW = 8, 4, 32, 48, 384
+HB = NC * CJ
+TW = 160
+BIG = 1024
+
+SCRATCH = {
+    "abuf": ("sbuf", [128, 1024], "bfloat16"),
+    "bbuf": ("sbuf", [128, 1024], "bfloat16"),
+    "lst": ("sbuf", [32, 16], "int32"),
+    "l4": ("sbuf", [128, 16], "int32"),
+    "off": ("sbuf", [128, 64], "uint16"),
+    "ta": ("sbuf", [128, 4 * TW], "bfloat16"),
+    "tb": ("sbuf", [128, 4 * HB], "bfloat16"),
+    "cac": ("sbuf", [128, TW], "float8_e4m3fn_x4"),
+    "cas": ("sbuf", [128, TW], "uint8"),
+    "cbc": ("sbuf", [128, HB], "float8_e4m3fn_x4"),
+    "cbs": ("sbuf", [128, HB], "uint8"),
+    "hxc": ("sbuf", [128, 2 * CI], "float8_e4m3fn_x4"),
+    "hys": ("sbuf", [128, 256], "uint8"),
+    "lac": ("sbuf", [128, 256], "float8_e4m3fn_x4"),
+    "las": ("sbuf", [128, 256], "uint8"),
+    "lbc": ("sbuf", [128, JW], "float8_e4m3fn_x4"),
+    "lbs": ("sbuf", [128, JW], "uint8"),
+    "ps": ("psum", [128, 2048], "float32"),
+    "p0": ("sbuf", [128, JW], "float32"),
+    "p1": ("sbuf", [128, JW], "float32"),
+    "y0": ("sbuf", [128, JW], "float32"),
+    "y1": ("sbuf", [128, JW], "float32"),
+    "pjl": ("sbuf", [32, 24], "int32"),
+    "pju": ("sbuf", [128, 24], "uint16"),
+    "pir": ("sbuf", [1, 128], "int32"),
+    "pib": ("sbuf", [128, 128], "int32"),
+    "pcol": ("sbuf", [128, 2], "float32"),
+    "wgt": ("sbuf", [128, 128], "float32"),
+    "eq": ("sbuf", [128, 256], "float32"),
+    "em": ("sbuf", [128, 256], "float32"),
+    "rs": ("sbuf", [128, 2], "float32"),
+    "inv": ("sbuf", [128, 2], "int32"),
+}
+SEMAPHORES = ["la", "lb", "ll", "lp", "gp", "gi", "vz", "v1", "v2", "gav", "gas", "qa", "gbv", "gbs", "qb", "vj", "ve", "vm",
+              "vr", "vi", "oc", "hx", "hy", "a0", "a1", "b1c", "b1s", "b2", "ls", "m0", "m1", "m2", "m3",
+              "c0", "c1", "c2", "c3", "o0", "o1", "st"]
+COPY = ActivationFunctionType.Copy
+
+
+def bits(engines):
+    m = 0
+    for e in engines:
+        m |= 1 << e
+    return m
+
+
+def move(topo, core, dsts, src, dst, engines, sem):
+    ids = []
+    for d in dsts:
+        rid, pid = topo.addr(d, core)
+        ids.append(DstId(rid=rid, pnc=pid))
+    return RemoteDMATransfer(dst_ids=ids, srcs=[src], dsts=[dst] * len(ids), dma_engine_mask=bits(engines), remote_sem=sem)
+
+
+def forwarders(topo, rank_core, side):
+    ok = [c for c in topo.cores_of(rank_core) if topo.die(c) != topo.die(rank_core)
+          and all(topo.may_write(c, d) for d in side)]
+    return ok[0], ok[1]
+
+
+def rank_program(g, core, T, topo):
+    cores = list(T.cores)
+    sides = [[c for c in cores if topo.host(c) == topo.host(cores[0])], [c for c in cores if topo.host(c) != topo.host(cores[0])]]
+    if T.rank_of(core) is None:
+        for h in range(2):
+            for c in range(NC):
+                fx, fy = forwarders(topo, sides[h][c], sides[h])
+                if core in (fx, fy):
+                    forward(g, core, T, topo, sides, h, c, core == fx)
+        return
+    h = 0 if core in sides[0] else 1
+    rank_core(g, core, T, topo, sides, h, sides[h].index(core))
+
+
+def a_plan(topo, me, fx, gx):
+    off = topo.engines(me, gx)
+    on = [e for e in topo.engines(me, fx) if e not in off]
+    return off[:4], off[4:8], on[:2], on[2:4]
+
+
+def forward(g, core, T, topo, sides, h, c, codes):
+    engines = topo.engines(core, sides[h][0])
+    for d in sides[h]:
+        engines = [e for e in engines if e in topo.engines(core, d)]
+    sem = T.sem["a%d" % (c // 2)]
+    if codes:
+        g.wait_ge(T.sem.hx, 6)
+        tr = move(topo, core, sides[h], T.hxc[:].bitcast(dt.uint8), T.lac[:, c * 64:c * 64 + 64].bitcast(dt.uint8), engines, sem)
+    else:
+        g.wait_ge(T.sem.hy, 6)
+        tr = move(topo, core, sides[h], T.hys[:, 96:160], T.las[:, c * 64:c * 64 + 64], engines, sem)
+    g.remote_dma_fused([tr], local_sem=T.sem.ls)
+    g.wait_ge(T.sem.ls, len(engines))
+
+
+def rank_core(g, me, T, topo, sides, h, c):
+    S = T.sem
+    V, A, X, Y = g.vector, g.scalar, g.tensor, g.sync
+    mine, r = sides[h], h * NC + c
+    partner = sides[1 - h][c]
+    ba = 96 if h == 0 else 0
+    own, oth = slice(h * HB, h * HB + HB), slice((1 - h) * HB, (1 - h) * HB + HB)
+
+    Y.dma_start(T.abuf[:], T.a[:]).then_inc(S.la, 16)
+    Y.dma_start(T.bbuf[:], T.b[:]).then_inc(S.lb, 16)
+    for i in range(2):
+        A.dma_start(T.lst[16 * i:16 * i + 16, 0:4], T.sa[:]).then_inc(S.ll, 16)
+        A.dma_start(T.lst[16 * i:16 * i + 16, 4:16], T.sb[:]).then_inc(S.ll, 16)
+    for i in range(2):
+        A.dma_start(T.pjl[16 * i:16 * i + 16, :], T.pj[:]).then_inc(S.lp, 16)
+
+    g.dma_start(T.pir[:], T.pi[:]).then_inc(S.gp, 16)
+    for b in range(4):
+        g.iota(T.pcol[32 * b:32 * b + 32, 0:2], [[64, 2]], (b % 2) * 128 + (b // 2) * 32, 1,
+               allow_small_or_imprecise_dtypes=True).then_inc(S.gi, 1)
+    g.wait_ge(S.gi, 4)
+    g.iota(T.wgt[:], [[1, 16], [16, 8]], -BIG, 0, allow_small_or_imprecise_dtypes=True).then_inc(S.gi, 1)
+    g.wait_ge(S.gi, 5)
+    g.wait_ge(S.gp, 16)
+    g.partition_broadcast(T.pib[:], T.pir[:], 128).then_inc(S.gi, 1)
+
+    V.memset(T.ta[:, (0 if h == 0 else 4 * 64):(4 * 96 if h == 0 else 4 * TW)], 0.0).then_inc(S.vz, 1)
+    V.wait_ge(S.ll, 64)
+    for b in range(4):
+        V.tensor_scalar(T.l4[32 * b:32 * b + 32, :], T.lst[:], 4, 0, AluOpType.mult, AluOpType.max).then_inc(S.v1, 1)
+    V.wait_ge(S.v1, 4)
+    for t in range(4):
+        V.tensor_scalar(T.off[:, 16 * t:16 * t + 16], T.l4[:], t, None, AluOpType.add).then_inc(S.v2, 1)
+    V.wait_ge(S.v2, 4)
+    A.wait_ge(S.v2, 4)
+    V.wait_ge(S.la, 16)
+    A.wait_ge(S.la, 16)
+
+    def pick(t, tile, first, n, win, o, sem):
+        out, in_ = tile[:, 4 * first + t:4 * (first + n):4], win[:, 0:1024].indirect(T.off[:, 16 * t + o:16 * t + o + n // 16])
+        if t < 2:
+            V.tensor_copy(out, in_).then_inc(sem, 1)
+        else:
+            A.activation(out, in_, COPY).then_inc(sem, 1)
+
+    for t in range(4):
+        pick(t, T.ta, ba, 2 * CI, T.abuf, 0, S.gav if t < 2 else S.gas)
+    V.wait_ge(S.vz, 1)
+    V.wait_ge(S.gav, 2)
+    V.wait_ge(S.gas, 2)
+    V.quantize_mx(T.cac[:], T.cas[:], T.ta[:]).then_inc(S.qa, 1)
+    V.wait_ge(S.lb, 16)
+    A.wait_ge(S.lb, 16)
+    for t in range(4):
+        pick(t, T.tb, 0, HB, T.bbuf, 4, S.gbv if t < 2 else S.gbs)
+    V.wait_ge(S.gbv, 2)
+    V.wait_ge(S.gbs, 2)
+    V.quantize_mx(T.cbc[:], T.cbs[:], T.tb[:]).then_inc(S.qb, 1)
+
+    Y.wait_ge(S.qb, 1)
+    Y.dma_start(T.lbc[:, r * CJ:r * CJ + CJ].bitcast(dt.uint8), T.cbc[:, c * CJ:c * CJ + CJ].bitcast(dt.uint8)).then_inc(S.oc, 16)
+    Y.dma_start(T.lbs[:, r * CJ:r * CJ + CJ], T.cbs[:, c * CJ:c * CJ + CJ]).then_inc(S.oc, 16)
+
+    fx, fy = forwarders(topo, me, mine)
+    gx, gy = forwarders(topo, partner, sides[1 - h])
+    e1, e2, e3, e4 = a_plan(topo, me, fx, gx)
+    ls = len(e1) + len(e2) + len(e3) + len(e4)
+    g.wait_ge(S.qa, 1)
+    tr = []
+    for s, cx, cy, ex, ey in ((1 - h, gx, gy, e1, e2), (h, fx, fy, e3, e4)):
+        k = ba + CI * s
+        tr.append(move(topo, me, [cx], T.cac[:, k:k + CI].bitcast(dt.uint8), T.hxc[:, CI * h:CI * h + CI].bitcast(dt.uint8), ex, S.hx))
+        tr.append(move(topo, me, [cy], T.cas[:, CI * s:CI * s + 128], T.hys[:, 128 * h:128 * h + 128], ey, S.hy))
+    g.remote_dma_fused(tr, local_sem=S.ls)
+
+    peers = [d for d in mine if d != me]
+    peers = [d for d in peers if not topo.mates(me, d) and not topo.same_plane(me, d)] + \
+            [d for d in peers if topo.mates(me, d) or topo.same_plane(me, d)]
+    off = topo.engines(me, peers[0])
+    g.wait_ge(S.qb, 1)
+    trc, trs = [], []
+    for i, d in enumerate(peers):
+        ec = off[0:4] if i == 0 else off[4 + 2 * i - 2:4 + 2 * i]
+        es = off[4:8] if i == 0 else off[2 * i - 2:2 * i]
+        k = mine.index(d)
+        trc.append(move(topo, me, [d], T.cbc[:, k * CJ:k * CJ + CJ].bitcast(dt.uint8), T.lbc[:, r * CJ:r * CJ + CJ].bitcast(dt.uint8), ec, S.b1c))
+        trs.append(move(topo, me, [d], T.cbs[:, k * CJ:k * CJ + CJ], T.lbs[:, r * CJ:r * CJ + CJ], es, S.b1s))
+    g.remote_dma_fused(trc, local_sem=S.ls)
+    g.remote_dma_fused(trs, local_sem=S.ls)
+    ls += 16
+
+    rid, pid = topo.addr(partner, me)
+    m = bits(topo.engines(me, partner))
+    g.wait_ge(S.oc, 32)
+    g.wait_ge(S.b1c, 8)
+    g.remote_dma(T.lbc[:, own].bitcast(dt.uint8), T.lbc[:, own].bitcast(dt.uint8), S.b2, S.ls, pid, rid, m)
+    g.wait_ge(S.b1s, 8)
+    g.remote_dma(T.lbs[:, own], T.lbs[:, own], S.b2, S.ls, pid, rid, m)
+    ls += 2 * len(topo.engines(me, partner))
+
+    V.wait_ge(S.lp, 32)
+    for b in range(4):
+        V.tensor_copy(T.pju[32 * b:32 * b + 32, :], T.pjl[:]).then_inc(S.vj, 1)
+    V.wait_ge(S.gi, 6)
+    for t in range(2):
+        V.tensor_scalar(T.eq[:, 128 * t:128 * t + 128], T.pib[:], T.pcol[:, t:t + 1], None, AluOpType.is_equal).then_inc(S.ve, 1)
+    V.wait_ge(S.ve, 2)
+    for t in range(2):
+        V.tensor_tensor(T.em[:, 128 * t:128 * t + 128], T.eq[:, 128 * t:128 * t + 128], T.wgt[:], AluOpType.mult).then_inc(S.vm, 1)
+    V.wait_ge(S.vm, 2)
+    for t in range(2):
+        V.tensor_reduce(T.rs[:, t:t + 1], T.em[:, 128 * t:128 * t + 128], AxisListType.X, AluOpType.add).then_inc(S.vr, 1)
+    V.wait_ge(S.vr, 2)
+    V.tensor_scalar(T.inv[:], T.rs[:], BIG, None, AluOpType.add).then_inc(S.vi, 1)
+
+    X.wait_ge(S.oc, 32)
+    X.wait_ge(S.b1c, 8)
+    X.wait_ge(S.b1s, 8)
+    for half, part in ((0, own), (1, oth)):
+        for t in range(2):
+            if half == 0:
+                X.wait_ge(S["a%d" % t], 32)
+            elif t == 0:
+                X.wait_ge(S.b2, 2 * len(topo.engines(partner, me)))
+            bank = 2 * half + t
+            X.matmul_mx(T.ps[:, 512 * bank:512 * bank + HB], T.lac[:, 128 * t:128 * t + 128], T.las[:, 128 * t:128 * t + 128],
+                        T.lbc[:, part], T.lbs[:, part], True, True).then_inc(S["m%d" % bank], 1)
+    for half, part in ((0, own), (1, oth)):
+        V.wait_ge(S["m%d" % (2 * half)], 1)
+        V.tensor_copy(T.p0[:, part], T.ps[:, 1024 * half:1024 * half + HB]).then_inc(S["c%d" % (2 * half)], 1)
+        A.wait_ge(S["m%d" % (2 * half + 1)], 1)
+        A.activation(T.p1[:, part], T.ps[:, 1024 * half + 512:1024 * half + 512 + HB], COPY).then_inc(S["c%d" % (2 * half + 1)], 1)
+
+    V.wait_ge(S.vj, 4)
+    A.wait_ge(S.vj, 4)
+    for t, p, y in ((0, T.p0, T.y0), (1, T.p1, T.y1)):
+        for q in (V, A):
+            q.wait_ge(S["c%d" % t], 1)
+            q.wait_ge(S["c%d" % (2 + t)], 1)
+        V.tensor_copy(y[:, 0:HB], p[:, 0:JW].indirect(T.pju[:, 0:12])).then_inc(S["o%d" % t], 1)
+        A.activation(y[:, HB:JW], p[:, 0:JW].indirect(T.pju[:, 12:24]), COPY).then_inc(S["o%d" % t], 1)
+    g.wait_ge(S.vi, 1)
+    for t, y in ((0, T.y0), (1, T.y1)):
+        g.wait_ge(S["o%d" % t], 2)
+        g.indirect_dma_start(T.y[:], IndirectOffsetOnAxis(ap=T.inv[:, t:t + 1], axis=0), y[:], None,
+                             bounds_check=127, oob_is_err=False).then_inc(S.st, 16)
+    g.wait_ge(S.ls, ls)
+    g.wait_ge(S.st, 32)

@@ -1,10 +1,9 @@
-from concourse.bass import DstId, RemoteDMATransfer, IndirectOffsetOnAxis
-from concourse.mybir import dt, AluOpType, AxisListType, ActivationFunctionType
+from concourse.bass import DstId, RemoteDMATransfer
+from concourse.mybir import dt, AluOpType, ActivationFunctionType
 
 N, NC, CI, CJ, JW = 8, 4, 32, 48, 384
 HB = NC * CJ
 TW = 160
-BIG = 1024
 
 SCRATCH = {
     "abuf": ("sbuf", [128, 1024], "bfloat16"),
@@ -18,31 +17,31 @@ SCRATCH = {
     "cas": ("sbuf", [128, TW], "uint8"),
     "cbc": ("sbuf", [128, HB], "float8_e4m3fn_x4"),
     "cbs": ("sbuf", [128, HB], "uint8"),
-    "hxc": ("sbuf", [128, 2 * CI], "float8_e4m3fn_x4"),
+    "hxc": ("sbuf", [128, CI], "float8_e4m3fn_x4"),
     "hys": ("sbuf", [128, 256], "uint8"),
     "lac": ("sbuf", [128, 256], "float8_e4m3fn_x4"),
     "las": ("sbuf", [128, 256], "uint8"),
     "lbc": ("sbuf", [128, JW], "float8_e4m3fn_x4"),
     "lbs": ("sbuf", [128, JW], "uint8"),
     "ps": ("psum", [128, 2048], "float32"),
-    "p0": ("sbuf", [128, JW], "float32"),
-    "p1": ("sbuf", [128, JW], "float32"),
-    "y0": ("sbuf", [128, JW], "float32"),
-    "y1": ("sbuf", [128, JW], "float32"),
-    "pjl": ("sbuf", [32, 24], "int32"),
-    "pju": ("sbuf", [128, 24], "uint16"),
-    "pir": ("sbuf", [1, 128], "int32"),
-    "pib": ("sbuf", [128, 128], "int32"),
-    "pcol": ("sbuf", [128, 2], "float32"),
-    "wgt": ("sbuf", [128, 128], "float32"),
-    "eq": ("sbuf", [128, 256], "float32"),
-    "em": ("sbuf", [128, 256], "float32"),
-    "rs": ("sbuf", [128, 2], "float32"),
-    "inv": ("sbuf", [128, 2], "int32"),
+    "prod": ("sbuf", [128, 768], "float32"),
+    "pick0": ("sbuf", [128, 192], "float32"),
+    "pick1": ("sbuf", [128, 192], "float32"),
+    "turned": ("sbuf", [128, 192], "float32"),
+    "fin": ("sbuf", [128, JW], "float32"),
+    "yout": ("sbuf", [128, JW], "float32"),
+    "lq": ("sbuf", [32, 32], "int32"),
+    "k1": ("sbuf", [32, 32], "int32"),
+    "k2": ("sbuf", [32, 32], "int32"),
+    "k3": ("sbuf", [32, 32], "int32"),
+    "k4": ("sbuf", [32, 32], "int32"),
+    "k5": ("sbuf", [32, 32], "int32"),
+    "ix": ("sbuf", [32, 48], "int32"),
+    "ixu": ("sbuf", [128, 48], "uint16"),
 }
-SEMAPHORES = ["la", "lb", "ll", "lp", "gp", "gi", "vz", "v1", "v2", "gav", "gas", "qa", "gbv", "gbs", "qb", "vj", "ve", "vm",
-              "vr", "vi", "oc", "hx", "hy", "a0", "a1", "b1c", "b1s", "b2", "ls", "m0", "m1", "m2", "m3",
-              "c0", "c1", "c2", "c3", "o0", "o1", "st"]
+SEMAPHORES = ["la", "lb", "ll", "lp", "vz", "v1", "v2", "gav", "gas", "qa", "gbv", "gbs", "qb", "vx",
+              "oc", "hx", "hy", "aa", "b1c", "b1s", "b2", "ls", "m0", "m1", "m2", "m3",
+              "cp", "g0", "g1", "tt", "ft", "out", "st"]
 COPY = ActivationFunctionType.Copy
 
 
@@ -62,9 +61,9 @@ def move(topo, core, dsts, src, dst, engines, sem):
 
 
 def forwarders(topo, rank_core, side):
-    ok = [c for c in topo.cores_of(rank_core) if topo.die(c) != topo.die(rank_core)
-          and all(topo.may_write(c, d) for d in side)]
-    return ok[0], ok[1]
+    ok = [c for c in topo.cores_of(rank_core) if c != rank_core and all(topo.may_write(c, d) for d in side)]
+    ok = [c for c in ok if topo.die(c) == topo.die(rank_core)] + [c for c in ok if topo.die(c) != topo.die(rank_core)]
+    return ok[:3]
 
 
 def rank_program(g, core, T, topo):
@@ -73,9 +72,9 @@ def rank_program(g, core, T, topo):
     if T.rank_of(core) is None:
         for h in range(2):
             for c in range(NC):
-                fx, fy = forwarders(topo, sides[h][c], sides[h])
-                if core in (fx, fy):
-                    forward(g, core, T, topo, sides, h, c, core == fx)
+                fw = forwarders(topo, sides[h][c], sides[h])
+                if core in fw:
+                    forward(g, core, T, topo, sides, h, c, fw.index(core))
         return
     h = 0 if core in sides[0] else 1
     rank_core(g, core, T, topo, sides, h, sides[h].index(core))
@@ -87,17 +86,17 @@ def a_plan(topo, me, fx, gx):
     return off[:4], off[4:8], on[:2], on[2:4]
 
 
-def forward(g, core, T, topo, sides, h, c, codes):
+def forward(g, core, T, topo, sides, h, c, role):
     engines = topo.engines(core, sides[h][0])
     for d in sides[h]:
         engines = [e for e in engines if e in topo.engines(core, d)]
-    sem = T.sem["a%d" % (c // 2)]
-    if codes:
-        g.wait_ge(T.sem.hx, 6)
-        tr = move(topo, core, sides[h], T.hxc[:].bitcast(dt.uint8), T.lac[:, c * 64:c * 64 + 64].bitcast(dt.uint8), engines, sem)
+    if role < 2:
+        g.wait_ge(T.sem.hx, 2 if role == 0 else 4)
+        k = c * 64 + CI * (h if role == 0 else 1 - h)
+        tr = move(topo, core, sides[h], T.hxc[:].bitcast(dt.uint8), T.lac[:, k:k + CI].bitcast(dt.uint8), engines, T.sem.aa)
     else:
         g.wait_ge(T.sem.hy, 6)
-        tr = move(topo, core, sides[h], T.hys[:, 96:160], T.las[:, c * 64:c * 64 + 64], engines, sem)
+        tr = move(topo, core, sides[h], T.hys[:, 96:160], T.las[:, c * 64:c * 64 + 64], engines, T.sem.aa)
     g.remote_dma_fused([tr], local_sem=T.sem.ls)
     g.wait_ge(T.sem.ls, len(engines))
 
@@ -108,25 +107,16 @@ def rank_core(g, me, T, topo, sides, h, c):
     mine, r = sides[h], h * NC + c
     partner = sides[1 - h][c]
     ba = 96 if h == 0 else 0
-    own, oth = slice(h * HB, h * HB + HB), slice((1 - h) * HB, (1 - h) * HB + HB)
+    own = slice(h * HB, h * HB + HB)
 
+    for i, q in ((0, Y), (1, A)):
+        q.dma_start(T.lst[16 * i:16 * i + 16, 0:4], T.sa[:]).then_inc(S.ll, 16)
+        q.dma_start(T.lst[16 * i:16 * i + 16, 4:16], T.sb[:]).then_inc(S.ll, 16)
     Y.dma_start(T.abuf[:], T.a[:]).then_inc(S.la, 16)
     Y.dma_start(T.bbuf[:], T.b[:]).then_inc(S.lb, 16)
     for i in range(2):
-        A.dma_start(T.lst[16 * i:16 * i + 16, 0:4], T.sa[:]).then_inc(S.ll, 16)
-        A.dma_start(T.lst[16 * i:16 * i + 16, 4:16], T.sb[:]).then_inc(S.ll, 16)
-    for i in range(2):
-        A.dma_start(T.pjl[16 * i:16 * i + 16, :], T.pj[:]).then_inc(S.lp, 16)
-
-    g.dma_start(T.pir[:], T.pi[:]).then_inc(S.gp, 16)
-    for b in range(4):
-        g.iota(T.pcol[32 * b:32 * b + 32, 0:2], [[64, 2]], (b % 2) * 128 + (b // 2) * 32, 1,
-               allow_small_or_imprecise_dtypes=True).then_inc(S.gi, 1)
-    g.wait_ge(S.gi, 4)
-    g.iota(T.wgt[:], [[1, 16], [16, 8]], -BIG, 0, allow_small_or_imprecise_dtypes=True).then_inc(S.gi, 1)
-    g.wait_ge(S.gi, 5)
-    g.wait_ge(S.gp, 16)
-    g.partition_broadcast(T.pib[:], T.pir[:], 128).then_inc(S.gi, 1)
+        A.dma_start(T.lq[16 * i:16 * i + 16, 0:24], T.pj[:]).then_inc(S.lp, 16)
+        A.dma_start(T.lq[16 * i:16 * i + 16, 24:32], T.pi[:]).then_inc(S.lp, 16)
 
     V.memset(T.ta[:, (0 if h == 0 else 4 * 64):(4 * 96 if h == 0 else 4 * TW)], 0.0).then_inc(S.vz, 1)
     V.wait_ge(S.ll, 64)
@@ -165,15 +155,15 @@ def rank_core(g, me, T, topo, sides, h, c):
     Y.dma_start(T.lbc[:, r * CJ:r * CJ + CJ].bitcast(dt.uint8), T.cbc[:, c * CJ:c * CJ + CJ].bitcast(dt.uint8)).then_inc(S.oc, 16)
     Y.dma_start(T.lbs[:, r * CJ:r * CJ + CJ], T.cbs[:, c * CJ:c * CJ + CJ]).then_inc(S.oc, 16)
 
-    fx, fy = forwarders(topo, me, mine)
-    gx, gy = forwarders(topo, partner, sides[1 - h])
-    e1, e2, e3, e4 = a_plan(topo, me, fx, gx)
+    fo, _fp, fs = forwarders(topo, me, mine)
+    _go, gp, gs = forwarders(topo, partner, sides[1 - h])
+    e1, e2, e3, e4 = a_plan(topo, me, fo, gp)
     ls = len(e1) + len(e2) + len(e3) + len(e4)
     g.wait_ge(S.qa, 1)
     tr = []
-    for s, cx, cy, ex, ey in ((1 - h, gx, gy, e1, e2), (h, fx, fy, e3, e4)):
+    for s, cx, cy, ex, ey in ((1 - h, gp, gs, e1, e2), (h, fo, fs, e3, e4)):
         k = ba + CI * s
-        tr.append(move(topo, me, [cx], T.cac[:, k:k + CI].bitcast(dt.uint8), T.hxc[:, CI * h:CI * h + CI].bitcast(dt.uint8), ex, S.hx))
+        tr.append(move(topo, me, [cx], T.cac[:, k:k + CI].bitcast(dt.uint8), T.hxc[:].bitcast(dt.uint8), ex, S.hx))
         tr.append(move(topo, me, [cy], T.cas[:, CI * s:CI * s + 128], T.hys[:, 128 * h:128 * h + 128], ey, S.hy))
     g.remote_dma_fused(tr, local_sem=S.ls)
 
@@ -201,52 +191,62 @@ def rank_core(g, me, T, topo, sides, h, c):
     g.wait_ge(S.b1s, 8)
     g.remote_dma(T.lbs[:, own], T.lbs[:, own], S.b2, S.ls, pid, rid, m)
     ls += 2 * len(topo.engines(me, partner))
+    g.wait_ge(S.ls, ls)
 
-    V.wait_ge(S.lp, 32)
+    V.wait_ge(S.lp, 64)
+    V.tensor_scalar(T.k1[:], T.lq[:], 96, None, AluOpType.bitwise_and).then_inc(S.vx, 1)
+    V.tensor_scalar(T.k2[:], T.lq[:], 384, None, AluOpType.bitwise_and).then_inc(S.vx, 1)
+    V.wait_ge(S.vx, 2)
+    V.tensor_scalar(T.k3[:], T.k2[:], -0.75, None, AluOpType.mult).then_inc(S.vx, 1)
+    V.wait_ge(S.vx, 3)
+    V.tensor_tensor(T.k4[:], T.lq[:], T.k3[:], AluOpType.add).then_inc(S.vx, 1)
+    V.wait_ge(S.vx, 4)
+    V.tensor_tensor(T.k5[:], T.k4[:], T.k1[:], AluOpType.add).then_inc(S.vx, 1)
+    V.wait_ge(S.vx, 5)
+    V.tensor_tensor(T.ix[:, 0:24], T.k5[:, 0:24], T.k1[:, 0:24], AluOpType.add).then_inc(S.vx, 1)
+    for t in range(3):
+        for u in range(2):
+            V.tensor_scalar(T.ix[:, 24 + 2 * t + u:48:6], T.k5[:, 24 + u:32:2], 256 * t, None, AluOpType.add).then_inc(S.vx, 1)
+    V.wait_ge(S.vx, 12)
     for b in range(4):
-        V.tensor_copy(T.pju[32 * b:32 * b + 32, :], T.pjl[:]).then_inc(S.vj, 1)
-    V.wait_ge(S.gi, 6)
-    for t in range(2):
-        V.tensor_scalar(T.eq[:, 128 * t:128 * t + 128], T.pib[:], T.pcol[:, t:t + 1], None, AluOpType.is_equal).then_inc(S.ve, 1)
-    V.wait_ge(S.ve, 2)
-    for t in range(2):
-        V.tensor_tensor(T.em[:, 128 * t:128 * t + 128], T.eq[:, 128 * t:128 * t + 128], T.wgt[:], AluOpType.mult).then_inc(S.vm, 1)
-    V.wait_ge(S.vm, 2)
-    for t in range(2):
-        V.tensor_reduce(T.rs[:, t:t + 1], T.em[:, 128 * t:128 * t + 128], AxisListType.X, AluOpType.add).then_inc(S.vr, 1)
-    V.wait_ge(S.vr, 2)
-    V.tensor_scalar(T.inv[:], T.rs[:], BIG, None, AluOpType.add).then_inc(S.vi, 1)
+        V.tensor_copy(T.ixu[32 * b:32 * b + 32, :], T.ix[:]).then_inc(S.vx, 1)
+    V.wait_ge(S.vx, 16)
+    A.wait_ge(S.vx, 16)
 
+    e, l = (0, 1) if h == 0 else (2, 0)
     X.wait_ge(S.oc, 32)
     X.wait_ge(S.b1c, 8)
     X.wait_ge(S.b1s, 8)
-    for half, part in ((0, own), (1, oth)):
-        for t in range(2):
-            if half == 0:
-                X.wait_ge(S["a%d" % t], 32)
-            elif t == 0:
-                X.wait_ge(S.b2, 2 * len(topo.engines(partner, me)))
-            bank = 2 * half + t
-            X.matmul_mx(T.ps[:, 512 * bank:512 * bank + HB], T.lac[:, 128 * t:128 * t + 128], T.las[:, 128 * t:128 * t + 128],
-                        T.lbc[:, part], T.lbs[:, part], True, True).then_inc(S["m%d" % bank], 1)
-    for half, part in ((0, own), (1, oth)):
-        V.wait_ge(S["m%d" % (2 * half)], 1)
-        V.tensor_copy(T.p0[:, part], T.ps[:, 1024 * half:1024 * half + HB]).then_inc(S["c%d" % (2 * half)], 1)
-        A.wait_ge(S["m%d" % (2 * half + 1)], 1)
-        A.activation(T.p1[:, part], T.ps[:, 1024 * half + 512:1024 * half + 512 + HB], COPY).then_inc(S["c%d" % (2 * half + 1)], 1)
+    X.wait_ge(S.aa, 96)
+    for bank, t, x, w in ((0, e, 0, 256), (1, l, 0, 256), (2, l + 1, 0, 128), (3, l + 1, 128, 128)):
+        if bank == 1:
+            X.wait_ge(S.b2, 2 * len(topo.engines(partner, me)))
+        X.matmul_mx(T.ps[:, 512 * bank:512 * bank + w], T.lbc[:, 128 * t:128 * t + 128], T.lbs[:, 128 * t:128 * t + 128],
+                    T.lac[:, x:x + w], T.las[:, x:x + w], True, True).then_inc(S["m%d" % bank], 1)
+        A_or_V = A.activation if bank in (0, 2) else V.tensor_copy
+        (A if bank in (0, 2) else V).wait_ge(S["m%d" % bank], 1)
+        args = (T.prod[:, 256 * t + x:256 * t + x + w], T.ps[:, 512 * bank:512 * bank + w])
+        (A_or_V(*args, COPY) if bank in (0, 2) else A_or_V(*args)).then_inc(S.cp, 1)
 
-    V.wait_ge(S.vj, 4)
-    A.wait_ge(S.vj, 4)
-    for t, p, y in ((0, T.p0, T.y0), (1, T.p1, T.y1)):
-        for q in (V, A):
-            q.wait_ge(S["c%d" % t], 1)
-            q.wait_ge(S["c%d" % (2 + t)], 1)
-        V.tensor_copy(y[:, 0:HB], p[:, 0:JW].indirect(T.pju[:, 0:12])).then_inc(S["o%d" % t], 1)
-        A.activation(y[:, HB:JW], p[:, 0:JW].indirect(T.pju[:, 12:24]), COPY).then_inc(S["o%d" % t], 1)
-    g.wait_ge(S.vi, 1)
-    for t, y in ((0, T.y0), (1, T.y1)):
-        g.wait_ge(S["o%d" % t], 2)
-        g.indirect_dma_start(T.y[:], IndirectOffsetOnAxis(ap=T.inv[:, t:t + 1], axis=0), y[:], None,
-                             bounds_check=127, oob_is_err=False).then_inc(S.st, 16)
-    g.wait_ge(S.ls, ls)
-    g.wait_ge(S.st, 32)
+    for q in (V, A):
+        q.wait_ge(S.cp, 4)
+    win = T.prod[:, 0:768]
+    V.tensor_copy(T.pick1[:], win.indirect(T.ixu[:, 36:48])).then_inc(S.g1, 1)
+    A.activation(T.pick0[:], win.indirect(T.ixu[:, 24:36]), COPY).then_inc(S.g0, 1)
+    V.wait_ge(S.g1, 1)
+    V.transpose(T.turned[:], T.pick1[:]).then_inc(S.tt, 1)
+    A.wait_ge(S.tt, 1)
+    V.wait_ge(S.g0, 1)
+    for b in range(2):
+        for a in range(4):
+            V.transpose(T.fin[32 * b:32 * b + 32, 96 * a:96 * a + 96], T.pick0[32 * a:32 * a + 32, 96 * b:96 * b + 96]).then_inc(S.ft, 1)
+            A.activation(T.fin[32 * b + 64:32 * b + 96, 96 * a:96 * a + 96], T.turned[32 * a:32 * a + 32, 96 * b:96 * b + 96],
+                         COPY).then_inc(S.ft, 1)
+
+    for q in (V, A):
+        q.wait_ge(S.ft, 16)
+    V.tensor_copy(T.yout[:, 0:192], T.fin[:, 0:JW].indirect(T.ixu[:, 0:12])).then_inc(S.out, 1)
+    A.activation(T.yout[:, 192:JW], T.fin[:, 0:JW].indirect(T.ixu[:, 12:24]), COPY).then_inc(S.out, 1)
+    Y.wait_ge(S.out, 2)
+    Y.dma_start(T.y[:], T.yout[:]).then_inc(S.st, 16)
+    Y.wait_ge(S.st, 16)

from concourse.bass import DstId, RemoteDMATransfer
from concourse.mybir import dt, AluOpType, ActivationFunctionType

N, NC, CI, CJ, JW = 8, 4, 32, 48, 384
HB = NC * CJ
TW = 160

SCRATCH = {
    "abuf": ("sbuf", [128, 1024], "bfloat16"),
    "bbuf": ("sbuf", [128, 1024], "bfloat16"),
    "lst": ("sbuf", [32, 16], "int32"),
    "l4": ("sbuf", [128, 16], "int32"),
    "off": ("sbuf", [128, 64], "uint16"),
    "ta": ("sbuf", [128, 4 * TW], "bfloat16"),
    "tb": ("sbuf", [128, 4 * HB], "bfloat16"),
    "cac": ("sbuf", [128, TW], "float8_e4m3fn_x4"),
    "cas": ("sbuf", [128, TW], "uint8"),
    "cbc": ("sbuf", [128, HB], "float8_e4m3fn_x4"),
    "cbs": ("sbuf", [128, HB], "uint8"),
    "hxc": ("sbuf", [128, CI], "float8_e4m3fn_x4"),
    "hys": ("sbuf", [128, 256], "uint8"),
    "lac": ("sbuf", [128, 256], "float8_e4m3fn_x4"),
    "las": ("sbuf", [128, 256], "uint8"),
    "lbc": ("sbuf", [128, JW], "float8_e4m3fn_x4"),
    "lbs": ("sbuf", [128, JW], "uint8"),
    "ps": ("psum", [128, 2048], "float32"),
    "prod": ("sbuf", [128, 768], "float32"),
    "pick0": ("sbuf", [128, 192], "float32"),
    "pick1": ("sbuf", [128, 192], "float32"),
    "turned": ("sbuf", [128, 192], "float32"),
    "fin": ("sbuf", [128, JW], "float32"),
    "yout": ("sbuf", [128, JW], "float32"),
    "lq": ("sbuf", [32, 32], "int32"),
    "k1": ("sbuf", [32, 32], "int32"),
    "k2": ("sbuf", [32, 32], "int32"),
    "k3": ("sbuf", [32, 32], "int32"),
    "k4": ("sbuf", [32, 32], "int32"),
    "k5": ("sbuf", [32, 32], "int32"),
    "ix": ("sbuf", [32, 48], "int32"),
    "ixu": ("sbuf", [128, 48], "uint16"),
}
SEMAPHORES = ["la", "lb", "ll", "lp", "vz", "v1", "v2", "gav", "gas", "qa", "gbv", "gbs", "qb", "vx",
              "oc", "hx", "hy", "aa", "b1c", "b1s", "b2", "ls", "m0", "m1", "m2", "m3",
              "cp", "g0", "g1", "tt", "ft", "out", "st"]
COPY = ActivationFunctionType.Copy


def bits(engines):
    m = 0
    for e in engines:
        m |= 1 << e
    return m


def move(topo, core, dsts, src, dst, engines, sem):
    ids = []
    for d in dsts:
        rid, pid = topo.addr(d, core)
        ids.append(DstId(rid=rid, pnc=pid))
    return RemoteDMATransfer(dst_ids=ids, srcs=[src], dsts=[dst] * len(ids), dma_engine_mask=bits(engines), remote_sem=sem)


def forwarders(topo, rank_core, side):
    ok = [c for c in topo.cores_of(rank_core) if c != rank_core and all(topo.may_write(c, d) for d in side)]
    ok = [c for c in ok if topo.die(c) == topo.die(rank_core)] + [c for c in ok if topo.die(c) != topo.die(rank_core)]
    return ok[:3]


def rank_program(g, core, T, topo):
    cores = list(T.cores)
    sides = [[c for c in cores if topo.host(c) == topo.host(cores[0])], [c for c in cores if topo.host(c) != topo.host(cores[0])]]
    if T.rank_of(core) is None:
        for h in range(2):
            for c in range(NC):
                fw = forwarders(topo, sides[h][c], sides[h])
                if core in fw:
                    forward(g, core, T, topo, sides, h, c, fw.index(core))
        return
    h = 0 if core in sides[0] else 1
    rank_core(g, core, T, topo, sides, h, sides[h].index(core))


def a_plan(topo, me, fx, gx):
    off = topo.engines(me, gx)
    on = [e for e in topo.engines(me, fx) if e not in off]
    return off[:4], off[4:8], on[:2], on[2:4]


def forward(g, core, T, topo, sides, h, c, role):
    engines = topo.engines(core, sides[h][0])
    for d in sides[h]:
        engines = [e for e in engines if e in topo.engines(core, d)]
    if role < 2:
        g.wait_ge(T.sem.hx, 2 if role == 0 else 4)
        k = c * 64 + CI * (h if role == 0 else 1 - h)
        tr = move(topo, core, sides[h], T.hxc[:].bitcast(dt.uint8), T.lac[:, k:k + CI].bitcast(dt.uint8), engines, T.sem.aa)
    else:
        g.wait_ge(T.sem.hy, 6)
        tr = move(topo, core, sides[h], T.hys[:, 96:160], T.las[:, c * 64:c * 64 + 64], engines, T.sem.aa)
    g.remote_dma_fused([tr], local_sem=T.sem.ls)
    g.wait_ge(T.sem.ls, len(engines))


def rank_core(g, me, T, topo, sides, h, c):
    S = T.sem
    V, A, X, Y = g.vector, g.scalar, g.tensor, g.sync
    mine, r = sides[h], h * NC + c
    partner = sides[1 - h][c]
    ba = 96 if h == 0 else 0
    own = slice(h * HB, h * HB + HB)

    for i, q in ((0, Y), (1, A)):
        q.dma_start(T.lst[16 * i:16 * i + 16, 0:4], T.sa[:]).then_inc(S.ll, 16)
        q.dma_start(T.lst[16 * i:16 * i + 16, 4:16], T.sb[:]).then_inc(S.ll, 16)
    Y.dma_start(T.abuf[:], T.a[:]).then_inc(S.la, 16)
    Y.dma_start(T.bbuf[:], T.b[:]).then_inc(S.lb, 16)
    for i in range(2):
        A.dma_start(T.lq[16 * i:16 * i + 16, 0:24], T.pj[:]).then_inc(S.lp, 16)
        A.dma_start(T.lq[16 * i:16 * i + 16, 24:32], T.pi[:]).then_inc(S.lp, 16)

    V.memset(T.ta[:, (0 if h == 0 else 4 * 64):(4 * 96 if h == 0 else 4 * TW)], 0.0).then_inc(S.vz, 1)
    V.wait_ge(S.ll, 64)
    for b in range(4):
        V.tensor_scalar(T.l4[32 * b:32 * b + 32, :], T.lst[:], 4, 0, AluOpType.mult, AluOpType.max).then_inc(S.v1, 1)
    V.wait_ge(S.v1, 4)
    for t in range(4):
        V.tensor_scalar(T.off[:, 16 * t:16 * t + 16], T.l4[:], t, None, AluOpType.add).then_inc(S.v2, 1)
    V.wait_ge(S.v2, 4)
    A.wait_ge(S.v2, 4)
    V.wait_ge(S.la, 16)
    A.wait_ge(S.la, 16)

    def pick(t, tile, first, n, win, o, sem):
        out, in_ = tile[:, 4 * first + t:4 * (first + n):4], win[:, 0:1024].indirect(T.off[:, 16 * t + o:16 * t + o + n // 16])
        if t < 2:
            V.tensor_copy(out, in_).then_inc(sem, 1)
        else:
            A.activation(out, in_, COPY).then_inc(sem, 1)

    for t in range(4):
        pick(t, T.ta, ba, 2 * CI, T.abuf, 0, S.gav if t < 2 else S.gas)
    V.wait_ge(S.vz, 1)
    V.wait_ge(S.gav, 2)
    V.wait_ge(S.gas, 2)
    V.quantize_mx(T.cac[:], T.cas[:], T.ta[:]).then_inc(S.qa, 1)
    V.wait_ge(S.lb, 16)
    A.wait_ge(S.lb, 16)
    for t in range(4):
        pick(t, T.tb, 0, HB, T.bbuf, 4, S.gbv if t < 2 else S.gbs)
    V.wait_ge(S.gbv, 2)
    V.wait_ge(S.gbs, 2)
    V.quantize_mx(T.cbc[:], T.cbs[:], T.tb[:]).then_inc(S.qb, 1)

    Y.wait_ge(S.qb, 1)
    Y.dma_start(T.lbc[:, r * CJ:r * CJ + CJ].bitcast(dt.uint8), T.cbc[:, c * CJ:c * CJ + CJ].bitcast(dt.uint8)).then_inc(S.oc, 16)
    Y.dma_start(T.lbs[:, r * CJ:r * CJ + CJ], T.cbs[:, c * CJ:c * CJ + CJ]).then_inc(S.oc, 16)

    fo, _fp, fs = forwarders(topo, me, mine)
    _go, gp, gs = forwarders(topo, partner, sides[1 - h])
    e1, e2, e3, e4 = a_plan(topo, me, fo, gp)
    ls = len(e1) + len(e2) + len(e3) + len(e4)
    g.wait_ge(S.qa, 1)
    tr = []
    for s, cx, cy, ex, ey in ((1 - h, gp, gs, e1, e2), (h, fo, fs, e3, e4)):
        k = ba + CI * s
        tr.append(move(topo, me, [cx], T.cac[:, k:k + CI].bitcast(dt.uint8), T.hxc[:].bitcast(dt.uint8), ex, S.hx))
        tr.append(move(topo, me, [cy], T.cas[:, CI * s:CI * s + 128], T.hys[:, 128 * h:128 * h + 128], ey, S.hy))
    g.remote_dma_fused(tr, local_sem=S.ls)

    peers = [d for d in mine if d != me]
    peers = [d for d in peers if not topo.mates(me, d) and not topo.same_plane(me, d)] + \
            [d for d in peers if topo.mates(me, d) or topo.same_plane(me, d)]
    off = topo.engines(me, peers[0])
    g.wait_ge(S.qb, 1)
    trc, trs = [], []
    for i, d in enumerate(peers):
        ec = off[0:4] if i == 0 else off[4 + 2 * i - 2:4 + 2 * i]
        es = off[4:8] if i == 0 else off[2 * i - 2:2 * i]
        k = mine.index(d)
        trc.append(move(topo, me, [d], T.cbc[:, k * CJ:k * CJ + CJ].bitcast(dt.uint8), T.lbc[:, r * CJ:r * CJ + CJ].bitcast(dt.uint8), ec, S.b1c))
        trs.append(move(topo, me, [d], T.cbs[:, k * CJ:k * CJ + CJ], T.lbs[:, r * CJ:r * CJ + CJ], es, S.b1s))
    g.remote_dma_fused(trc, local_sem=S.ls)
    g.remote_dma_fused(trs, local_sem=S.ls)
    ls += 16

    rid, pid = topo.addr(partner, me)
    m = bits(topo.engines(me, partner))
    g.wait_ge(S.oc, 32)
    g.wait_ge(S.b1c, 8)
    g.remote_dma(T.lbc[:, own].bitcast(dt.uint8), T.lbc[:, own].bitcast(dt.uint8), S.b2, S.ls, pid, rid, m)
    g.wait_ge(S.b1s, 8)
    g.remote_dma(T.lbs[:, own], T.lbs[:, own], S.b2, S.ls, pid, rid, m)
    ls += 2 * len(topo.engines(me, partner))
    g.wait_ge(S.ls, ls)

    V.wait_ge(S.lp, 64)
    V.tensor_scalar(T.k1[:], T.lq[:], 96, None, AluOpType.bitwise_and).then_inc(S.vx, 1)
    V.tensor_scalar(T.k2[:], T.lq[:], 384, None, AluOpType.bitwise_and).then_inc(S.vx, 1)
    V.wait_ge(S.vx, 2)
    V.tensor_scalar(T.k3[:], T.k2[:], -0.75, None, AluOpType.mult).then_inc(S.vx, 1)
    V.wait_ge(S.vx, 3)
    V.tensor_tensor(T.k4[:], T.lq[:], T.k3[:], AluOpType.add).then_inc(S.vx, 1)
    V.wait_ge(S.vx, 4)
    V.tensor_tensor(T.k5[:], T.k4[:], T.k1[:], AluOpType.add).then_inc(S.vx, 1)
    V.wait_ge(S.vx, 5)
    V.tensor_tensor(T.ix[:, 0:24], T.k5[:, 0:24], T.k1[:, 0:24], AluOpType.add).then_inc(S.vx, 1)
    for t in range(3):
        for u in range(2):
            V.tensor_scalar(T.ix[:, 24 + 2 * t + u:48:6], T.k5[:, 24 + u:32:2], 256 * t, None, AluOpType.add).then_inc(S.vx, 1)
    V.wait_ge(S.vx, 12)
    for b in range(4):
        V.tensor_copy(T.ixu[32 * b:32 * b + 32, :], T.ix[:]).then_inc(S.vx, 1)
    V.wait_ge(S.vx, 16)
    A.wait_ge(S.vx, 16)

    e, l = (0, 1) if h == 0 else (2, 0)
    X.wait_ge(S.oc, 32)
    X.wait_ge(S.b1c, 8)
    X.wait_ge(S.b1s, 8)
    X.wait_ge(S.aa, 96)
    for bank, t, x, w in ((0, e, 0, 256), (1, l, 0, 256), (2, l + 1, 0, 128), (3, l + 1, 128, 128)):
        if bank == 1:
            X.wait_ge(S.b2, 2 * len(topo.engines(partner, me)))
        X.matmul_mx(T.ps[:, 512 * bank:512 * bank + w], T.lbc[:, 128 * t:128 * t + 128], T.lbs[:, 128 * t:128 * t + 128],
                    T.lac[:, x:x + w], T.las[:, x:x + w], True, True).then_inc(S["m%d" % bank], 1)
        A_or_V = A.activation if bank in (0, 2) else V.tensor_copy
        (A if bank in (0, 2) else V).wait_ge(S["m%d" % bank], 1)
        args = (T.prod[:, 256 * t + x:256 * t + x + w], T.ps[:, 512 * bank:512 * bank + w])
        (A_or_V(*args, COPY) if bank in (0, 2) else A_or_V(*args)).then_inc(S.cp, 1)

    for q in (V, A):
        q.wait_ge(S.cp, 4)
    win = T.prod[:, 0:768]
    V.tensor_copy(T.pick1[:], win.indirect(T.ixu[:, 36:48])).then_inc(S.g1, 1)
    A.activation(T.pick0[:], win.indirect(T.ixu[:, 24:36]), COPY).then_inc(S.g0, 1)
    V.wait_ge(S.g1, 1)
    V.transpose(T.turned[:], T.pick1[:]).then_inc(S.tt, 1)
    A.wait_ge(S.tt, 1)
    V.wait_ge(S.g0, 1)
    for b in range(2):
        for a in range(4):
            V.transpose(T.fin[32 * b:32 * b + 32, 96 * a:96 * a + 96], T.pick0[32 * a:32 * a + 32, 96 * b:96 * b + 96]).then_inc(S.ft, 1)
            A.activation(T.fin[32 * b + 64:32 * b + 96, 96 * a:96 * a + 96], T.turned[32 * a:32 * a + 32, 96 * b:96 * b + 96],
                         COPY).then_inc(S.ft, 1)

    for q in (V, A):
        q.wait_ge(S.ft, 16)
    V.tensor_copy(T.yout[:, 0:192], T.fin[:, 0:JW].indirect(T.ixu[:, 0:12])).then_inc(S.out, 1)
    A.activation(T.yout[:, 192:JW], T.fin[:, 0:JW].indirect(T.ixu[:, 12:24]), COPY).then_inc(S.out, 1)
    Y.wait_ge(S.out, 2)
    Y.dma_start(T.y[:], T.yout[:]).then_inc(S.st, 16)
    Y.wait_ge(S.st, 16)
